import numpy as np
import ml_dtypes


def mxq(x, axis, fmt="e4m3"):
    dtype, down = {"e4m3": (ml_dtypes.float8_e4m3fn, 7), "e5m2": (ml_dtypes.float8_e5m2, 14)}[fmt]
    v = np.moveaxis(np.asarray(x, np.float32).astype(ml_dtypes.bfloat16).astype(np.float64), axis, -1)
    blocks = v.reshape(v.shape[:-1] + (-1, 32))
    amax = np.abs(blocks).max(-1, keepdims=True)
    byte = np.maximum(np.where(amax > 0, np.frexp(amax)[1] - 1 + 127, 0) - down, 1)
    scale = np.exp2(byte - 127.0)
    codes = (blocks / scale).astype(np.float32).astype(dtype).astype(np.float64)
    return np.moveaxis((codes * scale).reshape(v.shape), -1, axis)


WIDE = False


def mx_kscale(k):
    if not WIDE:
        return np.ones(k)
    levels = np.array([30, -30])
    if k % 512:
        return np.exp2(np.random.permutation(np.resize(levels, k // 32))).repeat(32)
    a = np.empty((k // 512, 16))
    for p in range(k // 512):
        a[p, :8] = np.random.permutation(np.resize(levels, 8))
        for g in range(8):
            far = levels[np.abs(levels - a[p, g]) >= 10]
            a[p, g + 8] = far[np.random.randint(len(far))]
    return np.exp2(a.ravel()).repeat(32)


def f64(x):
    return np.asarray(x).astype(np.float64)


def striped(idx):
    return np.tile(np.asarray(idx).reshape(-1, 16).T, (8, 1)).astype(np.uint16)


def unstriped(offs):
    return offs[:16].T.reshape(-1).astype(np.int64)


def striped8(idx):
    return np.asarray(idx).reshape(8, -1, 16).transpose(0, 2, 1).reshape(128, -1).astype(np.uint16)


def unstriped8(offs):
    return offs.reshape(8, 16, -1).transpose(0, 2, 1).reshape(8, -1).astype(np.int64)


def pick8(x, idx, run):
    r = np.arange(len(x))
    return x[r[:, None], idx[r % (8 * run) // run]]


E2M1 = np.array([0.0, 0.5, 1.0, 1.5, 2.0, 3.0, 4.0, 6.0, -0.0, -0.5, -1.0, -1.5, -2.0, -3.0, -4.0, -6.0])


def pack_weight(w, fmt):
    k, n = w.shape
    w = f64(np.asarray(w, np.float32).astype(ml_dtypes.bfloat16)).reshape(k // 32, 32, n)
    amax = np.abs(w).max(1)
    if fmt in ("e4m3", "e5m2"):
        byte = np.frexp(amax)[1] - 1 + 127 - (7 if fmt == "e4m3" else 14)
    else:
        mant, ex = np.frexp(amax / 6.0)
        byte = np.where(mant > 0.5, ex, ex - 1) + 127
    byte = np.clip(np.where(amax > 0, byte, 1), 1, 254)
    scaled = (w * np.exp2(127.0 - byte)[:, None, :]).reshape(k, n).astype(np.float32)
    by_word = np.ascontiguousarray(scaled.reshape(k // 512, 128, 4, n).transpose(0, 1, 3, 2))
    if fmt in ("e4m3", "e5m2"):
        words = by_word.astype(ml_dtypes.float8_e4m3fn if fmt == "e4m3" else ml_dtypes.float8_e5m2).view(np.uint8)
    else:
        c = by_word.astype(ml_dtypes.float4_e2m1fn).view(np.uint8) & 0xF
        words = (c[..., 0::2] | (c[..., 1::2] << 4)).reshape(k // 512, 128, 2 * n)
    return np.ascontiguousarray(words), np.ascontiguousarray(byte.astype(np.uint8).reshape(k // 512, 16, n))


def unpack_weight(words, scales, fmt):
    g, _, n = scales.shape
    words = np.ascontiguousarray(words).reshape(g, 128, n, -1)
    if fmt in ("e4m3", "e5m2"):
        vals = words.view(ml_dtypes.float8_e4m3fn if fmt == "e4m3" else ml_dtypes.float8_e5m2).astype(np.float64)
    else:
        nib = np.empty((g, 128, n, 4), np.uint8)
        nib[..., 0::2] = words & 0xF
        nib[..., 1::2] = words >> 4
        vals = E2M1[nib]
    vals = vals * np.repeat(np.exp2(scales.astype(np.float64) - 127.0), 8, axis=1)[..., None]
    return vals.transpose(0, 1, 3, 2).reshape(g * 512, n)


def e4m3fn_bytes(y):
    return np.clip(np.asarray(y, np.float64), -448.0, 448.0).astype(np.float32).astype(ml_dtypes.float8_e4m3fn).view(np.uint8)


def e4m3fn_values(b):
    return np.asarray(b, np.uint8).view(ml_dtypes.float8_e4m3fn).astype(np.float64)


K, T, J, R, V, N, E = 512, 1024, 256, 512, 1024, 256, 512


def setup_inputs():
    n = np.random.standard_normal
    idx = np.random.permutation(T)[:J]
    idx2 = np.stack([np.random.permutation(V)[:J] for _ in range(8)])
    idx3 = np.random.permutation(V)[:J]
    idx4 = np.random.permutation(E)[:J]
    fk = mx_kscale(K)
    fr = mx_kscale(R)
    xtp = pack_weight(n((K, T)) / fk[:, None], "e2m1")
    wp = pack_weight(n((K, R)) * 1 / np.sqrt(K) * fk[:, None], "e5m2")
    w2p = pack_weight(n((K, R)) * 1 / np.sqrt(K) * fk[:, None], "e4m3")
    wbp = pack_weight(n((R, N)) * 1 / np.sqrt(R) / fr[:, None], "e4m3")
    return {
        "xt_words": xtp[0],
        "xt_scales": xtp[1],
        "w_words": wp[0],
        "w_scales": wp[1],
        "w2_words": w2p[0],
        "w2_scales": w2p[1],
        "ca": e4m3fn_bytes(60.0 * n((R, V))),
        "sa": (np.random.uniform(0.004, 0.012, (R, 1)) * fr[:, None]).astype(np.float32),
        "sb": (np.random.uniform(0.004, 0.012, (R, 1)) * fr[:, None]).astype(np.float32),
        "wb_words": wbp[0],
        "wb_scales": wbp[1],
        "so": (np.random.uniform(0.5, 1.6, (N, 1))).astype(np.float32),
        "offs": striped(idx),
        "offs2": striped8(idx2),
        "offs3": striped(idx3),
        "offs4": striped(idx4),
    }


def reference(xt_words, xt_scales, w_words, w_scales, w2_words, w2_scales, ca, sa, sb, wb_words, wb_scales, so, offs, offs2, offs3, offs4):
    idx = unstriped(offs)
    idx2 = unstriped8(offs2)
    idx3 = unstriped(offs3)
    idx4 = unstriped(offs4)
    xtu = unpack_weight(xt_words, xt_scales, "e2m1")
    wu = unpack_weight(w_words, w_scales, "e5m2")
    w2u = unpack_weight(w2_words, w2_scales, "e4m3")
    wbu = unpack_weight(wb_words, wb_scales, "e4m3")
    xtidxg = xtu[:, idx]
    a = wu.T @ xtidxg
    b = w2u.T @ xtidxg
    ga = pick8(e4m3fn_values(ca), idx2, 64) * f64(sa)
    gb = e4m3fn_values(ca)[:, idx3] * f64(sb)
    hid = a * ga + b * gb
    hidq = mxq(hid, 0, "e4m3")
    p = wbu.T @ hidq
    y = np.zeros((N, E))
    y[:, idx4] = p * f64(so)
    return y

@@ -1,0 +1,200 @@
+from contextlib import ExitStack
+
+import concourse.mybir as mybir
+
+F32 = mybir.dt.float32
+BF16 = mybir.dt.bfloat16
+I32 = mybir.dt.int32
+U32 = mybir.dt.uint32
+U16 = mybir.dt.uint16
+U8 = mybir.dt.uint8
+FP8 = mybir.dt.float8_e4m3fn
+E4M3X4 = mybir.dt.float8_e4m3fn_x4
+E5M2X4 = mybir.dt.float8_e5m2_x4
+E2M1X4 = mybir.dt.float4_e2m1fn_x4
+COPY = mybir.ActivationFunctionType.Copy
+MULT = mybir.AluOpType.mult
+ADD = mybir.AluOpType.add
+
+K, T, J, R, V, N, E = 512, 1024, 256, 512, 1024, 256, 512
+P = 128
+PACK = 4
+HALF = 128
+CHUNK = 64
+
+FLOPS = 2 * (2 * K * R * J + R * N * J)
+
+
+def tile_list_groupandcommon_kernel(
+    tc, xt_words, xt_scales, w_words, w_scales, w2_words, w2_scales, ca, sa, sb,
+    wb_words, wb_scales, so, offs, offs2, offs3, offs4, out,
+):
+    nc = tc.nc
+    with ExitStack() as ctx:
+        sb_pool = ctx.enter_context(tc.tile_pool(name="sbuf", bufs=1))
+        psum = ctx.enter_context(tc.psum_pool(name="psum", bufs=1))
+
+        def tile(name, shape, dtype):
+            return sb_pool.tile(shape, dtype, name=name, align_bytes=64)
+
+        x_list = tile("x_list", [P, J // 16], U16)
+        group_lists = tile("group_lists", [P, J // 16], U16)
+        common_list = tile("common_list", [P, J // 16], U16)
+        page_list = tile("page_list", [P, J // 16], U16)
+
+        xt_plane = tile("xt_plane", [P, T], U8)
+        wb_plane = tile("wb_plane", [P, N], U8)
+        w_plane_raw = tile("w_plane_raw", [P, R], U8)
+        w2_plane_raw = tile("w2_plane_raw", [P, R], U8)
+        pages = [tile(f"page{c}", [P, E], F32) for c in range(N // P)]
+        for plane in (xt_plane, wb_plane, w_plane_raw, w2_plane_raw):
+            nc.vector.memset(plane[:].bitcast(I32), 0)
+        for page in pages:
+            nc.vector.memset(page[:], 0.0)
+
+        w_rows = tile("w_rows", [4, 4, R // 4], I32)
+        w2_rows = tile("w2_rows", [4, 4, R // 4], I32)
+        nc.scalar.dma_start(w_rows[:], w_scales[0].bitcast(I32).rearrange("(q r) c -> r q c", r=4))
+        nc.scalar.dma_start(w2_rows[:], w2_scales[0].bitcast(I32).rearrange("(q r) c -> r q c", r=4))
+
+        gates = [tile(f"gates{t}", [P, V], U8) for t in range(PACK)]
+        ca_rows = ca.rearrange("(p t) v -> t p v", t=PACK)
+        xt_codes = tile("xt_codes", [P, T], U16)
+        w_raw = tile("w_raw", [P, R], I32)
+        w2_raw = tile("w2_raw", [P, R], I32)
+        wb_codes = tile("wb_codes", [P, N], I32)
+        nc.sync.dma_start(group_lists[:], offs2)
+        nc.sync.dma_start(gates[0][:], ca_rows[0])
+        nc.sync.dma_start(common_list[:], offs3)
+        nc.sync.dma_start(x_list[:], offs)
+        nc.scalar.dma_start(xt_codes[:].bitcast(I32), xt_words[0].bitcast(I32))
+        for q in range(4):
+            nc.sync.dma_start(xt_plane[32 * q : 32 * q + 4, :].bitcast(I32), xt_scales[0, 4 * q : 4 * q + 4, :].bitcast(I32))
+        nc.scalar.dma_start(w_raw[:], w_words[0].rearrange("p c t -> p (c t)").bitcast(I32))
+        nc.sync.dma_start(gates[1][:], ca_rows[1])
+        nc.scalar.dma_start(w2_raw[:], w2_words[0].rearrange("p c t -> p (c t)").bitcast(I32))
+        for t in range(2, PACK):
+            nc.sync.dma_start(gates[t][:], ca_rows[t])
+
+        sa_t = tile("sa_t", [P, PACK], F32)
+        sb_t = tile("sb_t", [P, PACK], F32)
+        so_t = tile("so_t", [P, N // P], F32)
+        nc.gpsimd.dma_start(sa_t[:], sa.rearrange("(p t) o -> p (t o)", t=PACK))
+        nc.gpsimd.dma_start(sb_t[:], sb.rearrange("(p t) o -> p (t o)", t=PACK))
+        with nc.allow_non_contiguous_dma(reason="one weight a partition"):
+            nc.gpsimd.dma_start(so_t[:], so.rearrange("(c p) o -> p (c o)", p=P))
+
+        nc.sync.dma_start(wb_codes[:], wb_words[0].rearrange("p c t -> p (c t)").bitcast(I32))
+        nc.sync.dma_start(page_list[:], offs4)
+        for q in range(4):
+            nc.sync.dma_start(wb_plane[32 * q : 32 * q + 4, :].bitcast(I32), wb_scales[0, 4 * q : 4 * q + 4, :].bitcast(I32))
+
+        w_plane = tile("w_plane", [P, R], U8)
+        w2_plane = tile("w2_plane", [P, R], U8)
+        for rows, raw, plane in ((w_rows, w_plane_raw, w_plane), (w2_rows, w2_plane_raw, w2_plane)):
+            for q in range(4):
+                nc.vector.tensor_copy(raw[32 * q : 32 * q + 4, :].bitcast(I32), rows[:, q, :])
+            nc.vector.tensor_copy(
+                plane[:].rearrange("p (t m) -> p t m", t=PACK),
+                raw[:].rearrange("p (m t) -> p t m", t=PACK),
+            )
+
+        w_codes = tile("w_codes", [P, R], U32)
+        w2_codes = tile("w2_codes", [P, R], U32)
+        for raw, codes in ((w_raw, w_codes), (w2_raw, w2_codes)):
+            nc.scalar.copy(
+                codes[:].rearrange("p (t c i) -> p c t i", t=PACK, i=4),
+                raw[:].bitcast(U32).rearrange("p (c i t) -> p c t i", t=PACK, i=4),
+            )
+
+        ga = tile("ga", [P, PACK, J], F32)
+        gb = tile("gb", [P, PACK, J], F32)
+
+        def look_up(t, offsets, step, gate, name):
+            picked = tile(name, [P, J], U8)
+            nc.vector.tensor_copy(picked[:], gates[t][:].indirect(offsets[:]))
+            nc.scalar.activation(gate[:, t, :], picked[:].bitcast(FP8), COPY, scale=step[:, t : t + 1])
+
+        x_codes = tile("x_codes", [P, J], U16)
+        x_plane = tile("x_plane", [P, J], U8)
+        for t in range(PACK):
+            look_up(t, group_lists, sa_t, ga, f"picked_a{t}")
+            look_up(t, common_list, sb_t, gb, f"picked_b{t}")
+            if t == 0:
+                nc.vector.tensor_copy(x_codes[:], xt_codes[:].indirect(x_list[:]))
+                nc.vector.tensor_copy(x_plane[:], xt_plane[:].indirect(x_list[:]))
+
+        a_banks, b_banks = [], []
+        for h in range(J // HALF):
+            cols = slice(h * HALF, (h + 1) * HALF)
+            for banks, codes, plane, fmt, name in (
+                (a_banks, w_codes, w_plane, E5M2X4, "a"),
+                (b_banks, w2_codes, w2_plane, E4M3X4, "b"),
+            ):
+                bank = psum.tile([P, PACK, HALF], F32, name=f"{name}{h}")
+                banks.append(bank)
+                for t in range(PACK):
+                    feats = slice(t * P, (t + 1) * P)
+                    nc.tensor.matmul_mx(
+                        out=bank[:, t, :],
+                        lhsT=codes[:, feats].bitcast(fmt),
+                        lhsT_scale=plane[:, feats],
+                        rhs=x_codes[:, cols].bitcast(E2M1X4),
+                        rhs_scale=x_plane[:, cols],
+                        start=True,
+                        stop=True,
+                    )
+
+        chunks = J // CHUNK
+        first, second, hid = {}, {}, {}
+
+        def product(c, banks, gate, held, name):
+            h, lo = divmod(c * CHUNK, HALF)
+            held[c] = tile(f"{name}{c}", [P, PACK, CHUNK], F32)
+            nc.vector.tensor_tensor(
+                held[c][:], banks[h][:, :, lo : lo + CHUNK], gate[:, :, c * CHUNK : (c + 1) * CHUNK], MULT
+            )
+
+        def add_up(c):
+            hid[c] = tile(f"hid{c}", [P, CHUNK * PACK], BF16)
+            nc.vector.tensor_tensor(
+                hid[c][:].rearrange("p (c i t) -> p c t i", t=PACK, i=4),
+                first[c][:].rearrange("p t (c i) -> p c t i", i=4),
+                second[c][:].rearrange("p t (c i) -> p c t i", i=4),
+                ADD,
+            )
+
+        def finish(c):
+            hid_codes = tile(f"hid_codes{c}", [P, CHUNK], U32)
+            hid_plane = tile(f"hid_plane{c}", [P, CHUNK], U8)
+            nc.vector.quantize_mx(out=hid_codes[:].bitcast(E4M3X4), scales=hid_plane[:], in_=hid[c][:])
+            p_bank = psum.tile([P, N // P, CHUNK], F32, name=f"p{c}")
+            for n in range(N // P):
+                feats = slice(n * P, (n + 1) * P)
+                nc.tensor.matmul_mx(
+                    out=p_bank[:, n, :],
+                    lhsT=wb_codes[:, feats].bitcast(E4M3X4),
+                    lhsT_scale=wb_plane[:, feats],
+                    rhs=hid_codes[:].bitcast(E4M3X4),
+                    rhs_scale=hid_plane[:],
+                    start=True,
+                    stop=True,
+                )
+            p_rows = tile(f"p_rows{c}", [P, N // P, CHUNK], F32)
+            nc.vector.tensor_copy(p_rows[:], p_bank[:])
+            places = page_list[:, c * CHUNK // 16 : (c + 1) * CHUNK // 16]
+            for n in range(N // P):
+                nc.scalar.activation(pages[n][:].indirect(places), p_rows[:, n, :], COPY, scale=so_t[:, n : n + 1])
+
+        product(0, a_banks, ga, first, "first")
+        product(0, b_banks, gb, second, "second")
+        for c in range(chunks):
+            if c + 1 < chunks:
+                product(c + 1, a_banks, ga, first, "first")
+            add_up(c)
+            if c + 1 < chunks:
+                product(c + 1, b_banks, gb, second, "second")
+            finish(c)
+
+        nc.sync.dma_start(out[0:P, :], pages[0][:])
+        nc.scalar.dma_start(out[P : 2 * P, :], pages[1][:])

@@ -44,18 +44,15 @@ def tile_list_groupandcommon_kernel(
 
         xt_plane = tile("xt_plane", [P, T], U8)
         wb_plane = tile("wb_plane", [P, N], U8)
-        w_plane_raw = tile("w_plane_raw", [P, R], U8)
-        w2_plane_raw = tile("w2_plane_raw", [P, R], U8)
+        w_rows = tile("w_rows", [P, 4, R // 4], I32)
+        w2_rows = tile("w2_rows", [P, 4, R // 4], I32)
         pages = [tile(f"page{c}", [P, E], F32) for c in range(N // P)]
-        for plane in (xt_plane, wb_plane, w_plane_raw, w2_plane_raw):
-            nc.vector.memset(plane[:].bitcast(I32), 0)
+        nc.vector.memset(w_rows[:, 0, :], 0)
+        nc.vector.memset(w2_rows[:, 0, :], 0)
+        nc.vector.memset(xt_plane[:].bitcast(I32), 0)
+        nc.vector.memset(wb_plane[:].bitcast(I32), 0)
         for page in pages:
             nc.vector.memset(page[:], 0.0)
-
-        w_rows = tile("w_rows", [4, 4, R // 4], I32)
-        w2_rows = tile("w2_rows", [4, 4, R // 4], I32)
-        nc.scalar.dma_start(w_rows[:], w_scales[0].bitcast(I32).rearrange("(q r) c -> r q c", r=4))
-        nc.scalar.dma_start(w2_rows[:], w2_scales[0].bitcast(I32).rearrange("(q r) c -> r q c", r=4))
 
         gates = [tile(f"gates{t}", [P, V], U8) for t in range(PACK)]
         ca_rows = ca.rearrange("(p t) v -> t p v", t=PACK)
@@ -63,40 +60,46 @@ def tile_list_groupandcommon_kernel(
         w_raw = tile("w_raw", [P, R], I32)
         w2_raw = tile("w2_raw", [P, R], I32)
         wb_codes = tile("wb_codes", [P, N], I32)
-        nc.sync.dma_start(group_lists[:], offs2)
-        nc.sync.dma_start(gates[0][:], ca_rows[0])
-        nc.sync.dma_start(common_list[:], offs3)
-        nc.sync.dma_start(x_list[:], offs)
-        nc.scalar.dma_start(xt_codes[:].bitcast(I32), xt_words[0].bitcast(I32))
-        for q in range(4):
-            nc.sync.dma_start(xt_plane[32 * q : 32 * q + 4, :].bitcast(I32), xt_scales[0, 4 * q : 4 * q + 4, :].bitcast(I32))
-        nc.scalar.dma_start(w_raw[:], w_words[0].rearrange("p c t -> p (c t)").bitcast(I32))
-        nc.sync.dma_start(gates[1][:], ca_rows[1])
-        nc.scalar.dma_start(w2_raw[:], w2_words[0].rearrange("p c t -> p (c t)").bitcast(I32))
-        for t in range(2, PACK):
-            nc.sync.dma_start(gates[t][:], ca_rows[t])
-
         sa_t = tile("sa_t", [P, PACK], F32)
         sb_t = tile("sb_t", [P, PACK], F32)
         so_t = tile("so_t", [P, N // P], F32)
-        nc.gpsimd.dma_start(sa_t[:], sa.rearrange("(p t) o -> p (t o)", t=PACK))
-        nc.gpsimd.dma_start(sb_t[:], sb.rearrange("(p t) o -> p (t o)", t=PACK))
-        with nc.allow_non_contiguous_dma(reason="one weight a partition"):
-            nc.gpsimd.dma_start(so_t[:], so.rearrange("(c p) o -> p (c o)", p=P))
 
+        def load_plane(plane, scales):
+            for q in range(4):
+                nc.sync.dma_start(plane[32 * q : 32 * q + 4, :].bitcast(I32), scales[0, 4 * q : 4 * q + 4, :].bitcast(I32))
+
+        def load_rows(rows, scales):
+            nc.sync.dma_start(rows[0:4, :, :], scales[0].bitcast(I32).rearrange("(q r) c -> r q c", r=4))
+
+        nc.sync.dma_start(group_lists[:], offs2)
+        nc.sync.dma_start(gates[0][:], ca_rows[0])
+        nc.sync.dma_start(common_list[:], offs3)
+        nc.sync.dma_start(gates[1][:], ca_rows[1])
+        load_rows(w_rows, w_scales)
+        load_rows(w2_rows, w2_scales)
+        nc.sync.dma_start(x_list[:], offs)
+        nc.sync.dma_start(xt_codes[:].bitcast(I32), xt_words[0].bitcast(I32))
+        nc.sync.dma_start(w_raw[:], w_words[0].rearrange("p c t -> p (c t)").bitcast(I32))
+        nc.sync.dma_start(w2_raw[:], w2_words[0].rearrange("p c t -> p (c t)").bitcast(I32))
+        load_plane(xt_plane, xt_scales)
+        nc.sync.dma_start(sa_t[:], sa.rearrange("(p t) o -> p (t o)", t=PACK))
+        nc.sync.dma_start(sb_t[:], sb.rearrange("(p t) o -> p (t o)", t=PACK))
+        nc.sync.dma_start(gates[2][:], ca_rows[2])
+        nc.sync.dma_start(gates[3][:], ca_rows[3])
         nc.sync.dma_start(wb_codes[:], wb_words[0].rearrange("p c t -> p (c t)").bitcast(I32))
+        load_plane(wb_plane, wb_scales)
         nc.sync.dma_start(page_list[:], offs4)
-        for q in range(4):
-            nc.sync.dma_start(wb_plane[32 * q : 32 * q + 4, :].bitcast(I32), wb_scales[0, 4 * q : 4 * q + 4, :].bitcast(I32))
+        with nc.allow_non_contiguous_dma(reason="one weight a partition"):
+            nc.sync.dma_start(so_t[:], so.rearrange("(c p) o -> p (c o)", p=P))
 
         w_plane = tile("w_plane", [P, R], U8)
         w2_plane = tile("w2_plane", [P, R], U8)
-        for rows, raw, plane in ((w_rows, w_plane_raw, w_plane), (w2_rows, w2_plane_raw, w2_plane)):
-            for q in range(4):
-                nc.vector.tensor_copy(raw[32 * q : 32 * q + 4, :].bitcast(I32), rows[:, q, :])
-            nc.vector.tensor_copy(
+        for rows, plane in ((w_rows, w_plane), (w2_rows, w2_plane)):
+            for q in range(1, 4):
+                nc.vector.tensor_copy(rows[32 * q : 32 * q + 4, 0, :], rows[0:4, q, :])
+            nc.gpsimd.tensor_copy(
                 plane[:].rearrange("p (t m) -> p t m", t=PACK),
-                raw[:].rearrange("p (m t) -> p t m", t=PACK),
+                rows[:, 0, :].bitcast(U8).rearrange("p (m t) -> p t m", t=PACK),
             )
 
         w_codes = tile("w_codes", [P, R], U32)
@@ -120,7 +123,7 @@ def tile_list_groupandcommon_kernel(
         for t in range(PACK):
             look_up(t, group_lists, sa_t, ga, f"picked_a{t}")
             look_up(t, common_list, sb_t, gb, f"picked_b{t}")
-            if t == 0:
+            if t == 1:
                 nc.vector.tensor_copy(x_codes[:], xt_codes[:].indirect(x_list[:]))
                 nc.vector.tensor_copy(x_plane[:], xt_plane[:].indirect(x_list[:]))
 
@@ -158,9 +161,9 @@ def tile_list_groupandcommon_kernel(
         def add_up(c):
             hid[c] = tile(f"hid{c}", [P, CHUNK * PACK], BF16)
             nc.vector.tensor_tensor(
-                hid[c][:].rearrange("p (c i t) -> p c t i", t=PACK, i=4),
-                first[c][:].rearrange("p t (c i) -> p c t i", i=4),
-                second[c][:].rearrange("p t (c i) -> p c t i", i=4),
+                hid[c][:].rearrange("p (c i t) -> p c t i", t=PACK, i=2),
+                first[c][:].rearrange("p t (c i) -> p c t i", i=2),
+                second[c][:].rearrange("p t (c i) -> p c t i", i=2),
                 ADD,
             )
 
@@ -181,7 +184,10 @@ def tile_list_groupandcommon_kernel(
                     stop=True,
                 )
             p_rows = tile(f"p_rows{c}", [P, N // P, CHUNK], F32)
-            nc.vector.tensor_copy(p_rows[:], p_bank[:])
+            if c < 2:
+                nc.scalar.copy(p_rows[:], p_bank[:])
+            else:
+                nc.vector.tensor_copy(p_rows[:], p_bank[:])
             places = page_list[:, c * CHUNK // 16 : (c + 1) * CHUNK // 16]
             for n in range(N // P):
                 nc.scalar.activation(pages[n][:].indirect(places), p_rows[:, n, :], COPY, scale=so_t[:, n : n + 1])

@@ -74,17 +74,17 @@ def tile_list_groupandcommon_kernel(
         nc.sync.dma_start(group_lists[:], offs2)
         nc.sync.dma_start(gates[0][:], ca_rows[0])
         nc.sync.dma_start(common_list[:], offs3)
-        nc.sync.dma_start(gates[1][:], ca_rows[1])
         load_rows(w_rows, w_scales)
         load_rows(w2_rows, w2_scales)
+        nc.sync.dma_start(gates[1][:], ca_rows[1])
         nc.sync.dma_start(x_list[:], offs)
         nc.sync.dma_start(xt_codes[:].bitcast(I32), xt_words[0].bitcast(I32))
-        nc.sync.dma_start(w_raw[:], w_words[0].rearrange("p c t -> p (c t)").bitcast(I32))
-        nc.sync.dma_start(w2_raw[:], w2_words[0].rearrange("p c t -> p (c t)").bitcast(I32))
+        nc.gpsimd.dma_start(sa_t[:], sa.rearrange("(p t) o -> p (t o)", t=PACK))
+        nc.gpsimd.dma_start(sb_t[:], sb.rearrange("(p t) o -> p (t o)", t=PACK))
         load_plane(xt_plane, xt_scales)
-        nc.sync.dma_start(sa_t[:], sa.rearrange("(p t) o -> p (t o)", t=PACK))
-        nc.sync.dma_start(sb_t[:], sb.rearrange("(p t) o -> p (t o)", t=PACK))
+        nc.sync.dma_start(w_raw[:], w_words[0].rearrange("p c t -> p (c t)").bitcast(I32))
         nc.sync.dma_start(gates[2][:], ca_rows[2])
+        nc.sync.dma_start(w2_raw[:], w2_words[0].rearrange("p c t -> p (c t)").bitcast(I32))
         nc.sync.dma_start(gates[3][:], ca_rows[3])
         nc.sync.dma_start(wb_codes[:], wb_words[0].rearrange("p c t -> p (c t)").bitcast(I32))
         load_plane(wb_plane, wb_scales)
@@ -134,7 +134,7 @@ def tile_list_groupandcommon_kernel(
                 (a_banks, w_codes, w_plane, E5M2X4, "a"),
                 (b_banks, w2_codes, w2_plane, E4M3X4, "b"),
             ):
-                bank = psum.tile([P, PACK, HALF], F32, name=f"{name}{h}")
+                bank = psum.tile([P, PACK, HALF], F32, name=f"{name}{h}", tag=f"{name}{h}")
                 banks.append(bank)
                 for t in range(PACK):
                     feats = slice(t * P, (t + 1) * P)
@@ -171,11 +171,16 @@ def tile_list_groupandcommon_kernel(
             hid_codes = tile(f"hid_codes{c}", [P, CHUNK], U32)
             hid_plane = tile(f"hid_plane{c}", [P, CHUNK], U8)
             nc.vector.quantize_mx(out=hid_codes[:].bitcast(E4M3X4), scales=hid_plane[:], in_=hid[c][:])
-            p_bank = psum.tile([P, N // P, CHUNK], F32, name=f"p{c}")
+            last = c == chunks - 1
+            if last:
+                p_banks = [psum.tile([P, CHUNK], F32, name=f"p{c}{n}", tag=("p_last", "a0")[n])[:] for n in range(N // P)]
+            else:
+                p_bank = psum.tile([P, N // P, CHUNK], F32, name=f"p{c}")
+                p_banks = [p_bank[:, n, :] for n in range(N // P)]
             for n in range(N // P):
                 feats = slice(n * P, (n + 1) * P)
                 nc.tensor.matmul_mx(
-                    out=p_bank[:, n, :],
+                    out=p_banks[n],
                     lhsT=wb_codes[:, feats].bitcast(E4M3X4),
                     lhsT_scale=wb_plane[:, feats],
                     rhs=hid_codes[:].bitcast(E4M3X4),
@@ -184,7 +189,10 @@ def tile_list_groupandcommon_kernel(
                     stop=True,
                 )
             p_rows = tile(f"p_rows{c}", [P, N // P, CHUNK], F32)
-            if c < 2:
+            if last:
+                for n in range(N // P):
+                    nc.vector.tensor_copy(p_rows[:, n, :], p_banks[n])
+            elif c < 2:
                 nc.scalar.copy(p_rows[:], p_bank[:])
             else:
                 nc.vector.tensor_copy(p_rows[:], p_bank[:])

@@ -44,13 +44,11 @@ def tile_list_groupandcommon_kernel(
 
         xt_plane = tile("xt_plane", [P, T], U8)
         wb_plane = tile("wb_plane", [P, N], U8)
-        w_rows = tile("w_rows", [P, 4, R // 4], I32)
-        w2_rows = tile("w2_rows", [P, 4, R // 4], I32)
+        w_plane_raw = tile("w_plane_raw", [P, R], U8)
+        w2_plane_raw = tile("w2_plane_raw", [P, R], U8)
         pages = [tile(f"page{c}", [P, E], F32) for c in range(N // P)]
-        nc.vector.memset(w_rows[:, 0, :], 0)
-        nc.vector.memset(w2_rows[:, 0, :], 0)
-        nc.vector.memset(xt_plane[:].bitcast(I32), 0)
-        nc.vector.memset(wb_plane[:].bitcast(I32), 0)
+        for plane in (w_plane_raw, xt_plane, w2_plane_raw, wb_plane):
+            nc.vector.memset(plane[:].bitcast(I32), 0)
         for page in pages:
             nc.vector.memset(page[:], 0.0)
 
@@ -68,38 +66,33 @@ def tile_list_groupandcommon_kernel(
             for q in range(4):
                 nc.sync.dma_start(plane[32 * q : 32 * q + 4, :].bitcast(I32), scales[0, 4 * q : 4 * q + 4, :].bitcast(I32))
 
-        def load_rows(rows, scales):
-            nc.sync.dma_start(rows[0:4, :, :], scales[0].bitcast(I32).rearrange("(q r) c -> r q c", r=4))
-
         nc.sync.dma_start(group_lists[:], offs2)
         nc.sync.dma_start(gates[0][:], ca_rows[0])
         nc.sync.dma_start(common_list[:], offs3)
-        load_rows(w_rows, w_scales)
-        load_rows(w2_rows, w2_scales)
         nc.sync.dma_start(gates[1][:], ca_rows[1])
+        load_plane(w_plane_raw, w_scales)
         nc.sync.dma_start(x_list[:], offs)
         nc.sync.dma_start(xt_codes[:].bitcast(I32), xt_words[0].bitcast(I32))
-        nc.gpsimd.dma_start(sa_t[:], sa.rearrange("(p t) o -> p (t o)", t=PACK))
-        nc.gpsimd.dma_start(sb_t[:], sb.rearrange("(p t) o -> p (t o)", t=PACK))
         load_plane(xt_plane, xt_scales)
         nc.sync.dma_start(w_raw[:], w_words[0].rearrange("p c t -> p (c t)").bitcast(I32))
         nc.sync.dma_start(gates[2][:], ca_rows[2])
+        nc.sync.dma_start(sa_t[:], sa.rearrange("(p t) o -> p (t o)", t=PACK))
+        nc.sync.dma_start(sb_t[:], sb.rearrange("(p t) o -> p (t o)", t=PACK))
         nc.sync.dma_start(w2_raw[:], w2_words[0].rearrange("p c t -> p (c t)").bitcast(I32))
+        load_plane(w2_plane_raw, w2_scales)
         nc.sync.dma_start(gates[3][:], ca_rows[3])
+        with nc.allow_non_contiguous_dma(reason="one weight a partition"):
+            nc.sync.dma_start(so_t[:], so.rearrange("(c p) o -> p (c o)", p=P))
         nc.sync.dma_start(wb_codes[:], wb_words[0].rearrange("p c t -> p (c t)").bitcast(I32))
         load_plane(wb_plane, wb_scales)
         nc.sync.dma_start(page_list[:], offs4)
-        with nc.allow_non_contiguous_dma(reason="one weight a partition"):
-            nc.sync.dma_start(so_t[:], so.rearrange("(c p) o -> p (c o)", p=P))
 
         w_plane = tile("w_plane", [P, R], U8)
         w2_plane = tile("w2_plane", [P, R], U8)
-        for rows, plane in ((w_rows, w_plane), (w2_rows, w2_plane)):
-            for q in range(1, 4):
-                nc.vector.tensor_copy(rows[32 * q : 32 * q + 4, 0, :], rows[0:4, q, :])
+        for raw, plane in ((w_plane_raw, w_plane), (w2_plane_raw, w2_plane)):
             nc.gpsimd.tensor_copy(
                 plane[:].rearrange("p (t m) -> p t m", t=PACK),
-                rows[:, 0, :].bitcast(U8).rearrange("p (m t) -> p t m", t=PACK),
+                raw[:].rearrange("p (m t) -> p t m", t=PACK),
             )
 
         w_codes = tile("w_codes", [P, R], U32)
@@ -153,7 +146,7 @@ def tile_list_groupandcommon_kernel(
 
         def product(c, banks, gate, held, name):
             h, lo = divmod(c * CHUNK, HALF)
-            held[c] = tile(f"{name}{c}", [P, PACK, CHUNK], F32)
+            held[c] = sb_pool.tile([P, PACK, CHUNK], F32, name=f"{name}{c}", tag=name, bufs=2)
             nc.vector.tensor_tensor(
                 held[c][:], banks[h][:, :, lo : lo + CHUNK], gate[:, :, c * CHUNK : (c + 1) * CHUNK], MULT
             )

@@ -47,7 +47,7 @@ def tile_list_groupandcommon_kernel(
         w_plane_raw = tile("w_plane_raw", [P, R], U8)
         w2_plane_raw = tile("w2_plane_raw", [P, R], U8)
         pages = [tile(f"page{c}", [P, E], F32) for c in range(N // P)]
-        for plane in (w_plane_raw, xt_plane, w2_plane_raw, wb_plane):
+        for plane in (xt_plane, w_plane_raw, w2_plane_raw, wb_plane):
             nc.vector.memset(plane[:].bitcast(I32), 0)
         for page in pages:
             nc.vector.memset(page[:], 0.0)
@@ -62,25 +62,26 @@ def tile_list_groupandcommon_kernel(
         sb_t = tile("sb_t", [P, PACK], F32)
         so_t = tile("so_t", [P, N // P], F32)
 
-        def load_plane(plane, scales):
-            for q in range(4):
+        def load_plane(plane, scales, quarters=range(4)):
+            for q in quarters:
                 nc.sync.dma_start(plane[32 * q : 32 * q + 4, :].bitcast(I32), scales[0, 4 * q : 4 * q + 4, :].bitcast(I32))
 
         nc.sync.dma_start(group_lists[:], offs2)
         nc.sync.dma_start(gates[0][:], ca_rows[0])
         nc.sync.dma_start(common_list[:], offs3)
         nc.sync.dma_start(gates[1][:], ca_rows[1])
-        load_plane(w_plane_raw, w_scales)
         nc.sync.dma_start(x_list[:], offs)
         nc.sync.dma_start(xt_codes[:].bitcast(I32), xt_words[0].bitcast(I32))
-        load_plane(xt_plane, xt_scales)
-        nc.sync.dma_start(w_raw[:], w_words[0].rearrange("p c t -> p (c t)").bitcast(I32))
+        load_plane(xt_plane, xt_scales, range(0, 2))
         nc.sync.dma_start(gates[2][:], ca_rows[2])
+        nc.sync.dma_start(w_raw[:], w_words[0].rearrange("p c t -> p (c t)").bitcast(I32))
+        load_plane(xt_plane, xt_scales, range(2, 4))
+        nc.sync.dma_start(w2_raw[:], w2_words[0].rearrange("p c t -> p (c t)").bitcast(I32))
+        nc.sync.dma_start(gates[3][:], ca_rows[3])
         nc.sync.dma_start(sa_t[:], sa.rearrange("(p t) o -> p (t o)", t=PACK))
         nc.sync.dma_start(sb_t[:], sb.rearrange("(p t) o -> p (t o)", t=PACK))
-        nc.sync.dma_start(w2_raw[:], w2_words[0].rearrange("p c t -> p (c t)").bitcast(I32))
+        load_plane(w_plane_raw, w_scales)
         load_plane(w2_plane_raw, w2_scales)
-        nc.sync.dma_start(gates[3][:], ca_rows[3])
         with nc.allow_non_contiguous_dma(reason="one weight a partition"):
             nc.sync.dma_start(so_t[:], so.rearrange("(c p) o -> p (c o)", p=P))
         nc.sync.dma_start(wb_codes[:], wb_words[0].rearrange("p c t -> p (c t)").bitcast(I32))
@@ -90,10 +91,11 @@ def tile_list_groupandcommon_kernel(
         w_plane = tile("w_plane", [P, R], U8)
         w2_plane = tile("w2_plane", [P, R], U8)
         for raw, plane in ((w_plane_raw, w_plane), (w2_plane_raw, w2_plane)):
-            nc.gpsimd.tensor_copy(
-                plane[:].rearrange("p (t m) -> p t m", t=PACK),
-                raw[:].rearrange("p (m t) -> p t m", t=PACK),
-            )
+            for t in range(0, PACK, 2):
+                nc.gpsimd.tensor_copy(
+                    plane[:].rearrange("p (t m) -> p t m", t=PACK)[:, t : t + 2, :],
+                    raw[:].rearrange("p (m t) -> p t m", t=PACK)[:, t : t + 2, :],
+                )
 
         w_codes = tile("w_codes", [P, R], U32)
         w2_codes = tile("w2_codes", [P, R], U32)

from contextlib import ExitStack

import concourse.mybir as mybir

F32 = mybir.dt.float32
BF16 = mybir.dt.bfloat16
I32 = mybir.dt.int32
U32 = mybir.dt.uint32
U16 = mybir.dt.uint16
U8 = mybir.dt.uint8
FP8 = mybir.dt.float8_e4m3fn
E4M3X4 = mybir.dt.float8_e4m3fn_x4
E5M2X4 = mybir.dt.float8_e5m2_x4
E2M1X4 = mybir.dt.float4_e2m1fn_x4
COPY = mybir.ActivationFunctionType.Copy
MULT = mybir.AluOpType.mult
ADD = mybir.AluOpType.add

K, T, J, R, V, N, E = 512, 1024, 256, 512, 1024, 256, 512
P = 128
PACK = 4
HALF = 128
CHUNK = 64

FLOPS = 2 * (2 * K * R * J + R * N * J)


def tile_list_groupandcommon_kernel(
    tc, xt_words, xt_scales, w_words, w_scales, w2_words, w2_scales, ca, sa, sb,
    wb_words, wb_scales, so, offs, offs2, offs3, offs4, out,
):
    nc = tc.nc
    with ExitStack() as ctx:
        sb_pool = ctx.enter_context(tc.tile_pool(name="sbuf", bufs=1))
        psum = ctx.enter_context(tc.psum_pool(name="psum", bufs=1))

        def tile(name, shape, dtype):
            return sb_pool.tile(shape, dtype, name=name, align_bytes=64)

        x_list = tile("x_list", [P, J // 16], U16)
        group_lists = tile("group_lists", [P, J // 16], U16)
        common_list = tile("common_list", [P, J // 16], U16)
        page_list = tile("page_list", [P, J // 16], U16)

        xt_plane = tile("xt_plane", [P, T], U8)
        wb_plane = tile("wb_plane", [P, N], U8)
        w_plane_raw = tile("w_plane_raw", [P, R], U8)
        w2_plane_raw = tile("w2_plane_raw", [P, R], U8)
        pages = [tile(f"page{c}", [P, E], F32) for c in range(N // P)]
        for plane in (xt_plane, w_plane_raw, w2_plane_raw, wb_plane):
            nc.vector.memset(plane[:].bitcast(I32), 0)
        for page in pages:
            nc.vector.memset(page[:], 0.0)

        gates = [tile(f"gates{t}", [P, V], U8) for t in range(PACK)]
        ca_rows = ca.rearrange("(p t) v -> t p v", t=PACK)
        xt_codes = tile("xt_codes", [P, T], U16)
        w_raw = tile("w_raw", [P, R], I32)
        w2_raw = tile("w2_raw", [P, R], I32)
        wb_codes = tile("wb_codes", [P, N], I32)
        sa_t = tile("sa_t", [P, PACK], F32)
        sb_t = tile("sb_t", [P, PACK], F32)
        so_t = tile("so_t", [P, N // P], F32)

        def load_plane(plane, scales, quarters=range(4)):
            for q in quarters:
                nc.sync.dma_start(plane[32 * q : 32 * q + 4, :].bitcast(I32), scales[0, 4 * q : 4 * q + 4, :].bitcast(I32))

        nc.sync.dma_start(group_lists[:], offs2)
        nc.sync.dma_start(gates[0][:], ca_rows[0])
        nc.sync.dma_start(common_list[:], offs3)
        nc.sync.dma_start(gates[1][:], ca_rows[1])
        nc.sync.dma_start(x_list[:], offs)
        nc.sync.dma_start(xt_codes[:].bitcast(I32), xt_words[0].bitcast(I32))
        load_plane(xt_plane, xt_scales, range(0, 2))
        nc.sync.dma_start(gates[2][:], ca_rows[2])
        nc.sync.dma_start(w_raw[:], w_words[0].rearrange("p c t -> p (c t)").bitcast(I32))
        load_plane(xt_plane, xt_scales, range(2, 4))
        nc.sync.dma_start(w2_raw[:], w2_words[0].rearrange("p c t -> p (c t)").bitcast(I32))
        nc.sync.dma_start(gates[3][:], ca_rows[3])
        nc.sync.dma_start(sa_t[:], sa.rearrange("(p t) o -> p (t o)", t=PACK))
        nc.sync.dma_start(sb_t[:], sb.rearrange("(p t) o -> p (t o)", t=PACK))
        load_plane(w_plane_raw, w_scales)
        load_plane(w2_plane_raw, w2_scales)
        with nc.allow_non_contiguous_dma(reason="one weight a partition"):
            nc.sync.dma_start(so_t[:], so.rearrange("(c p) o -> p (c o)", p=P))
        nc.sync.dma_start(wb_codes[:], wb_words[0].rearrange("p c t -> p (c t)").bitcast(I32))
        load_plane(wb_plane, wb_scales)
        nc.sync.dma_start(page_list[:], offs4)

        w_plane = tile("w_plane", [P, R], U8)
        w2_plane = tile("w2_plane", [P, R], U8)
        for raw, plane in ((w_plane_raw, w_plane), (w2_plane_raw, w2_plane)):
            for t in range(0, PACK, 2):
                nc.gpsimd.tensor_copy(
                    plane[:].rearrange("p (t m) -> p t m", t=PACK)[:, t : t + 2, :],
                    raw[:].rearrange("p (m t) -> p t m", t=PACK)[:, t : t + 2, :],
                )

        w_codes = tile("w_codes", [P, R], U32)
        w2_codes = tile("w2_codes", [P, R], U32)
        for raw, codes in ((w_raw, w_codes), (w2_raw, w2_codes)):
            nc.scalar.copy(
                codes[:].rearrange("p (t c i) -> p c t i", t=PACK, i=4),
                raw[:].bitcast(U32).rearrange("p (c i t) -> p c t i", t=PACK, i=4),
            )

        ga = tile("ga", [P, PACK, J], F32)
        gb = tile("gb", [P, PACK, J], F32)

        def look_up(t, offsets, step, gate, name):
            picked = tile(name, [P, J], U8)
            nc.vector.tensor_copy(picked[:], gates[t][:].indirect(offsets[:]))
            nc.scalar.activation(gate[:, t, :], picked[:].bitcast(FP8), COPY, scale=step[:, t : t + 1])

        x_codes = tile("x_codes", [P, J], U16)
        x_plane = tile("x_plane", [P, J], U8)
        for t in range(PACK):
            look_up(t, group_lists, sa_t, ga, f"picked_a{t}")
            look_up(t, common_list, sb_t, gb, f"picked_b{t}")
            if t == 1:
                nc.vector.tensor_copy(x_codes[:], xt_codes[:].indirect(x_list[:]))
                nc.vector.tensor_copy(x_plane[:], xt_plane[:].indirect(x_list[:]))

        a_banks, b_banks = [], []
        for h in range(J // HALF):
            cols = slice(h * HALF, (h + 1) * HALF)
            for banks, codes, plane, fmt, name in (
                (a_banks, w_codes, w_plane, E5M2X4, "a"),
                (b_banks, w2_codes, w2_plane, E4M3X4, "b"),
            ):
                bank = psum.tile([P, PACK, HALF], F32, name=f"{name}{h}", tag=f"{name}{h}")
                banks.append(bank)
                for t in range(PACK):
                    feats = slice(t * P, (t + 1) * P)
                    nc.tensor.matmul_mx(
                        out=bank[:, t, :],
                        lhsT=codes[:, feats].bitcast(fmt),
                        lhsT_scale=plane[:, feats],
                        rhs=x_codes[:, cols].bitcast(E2M1X4),
                        rhs_scale=x_plane[:, cols],
                        start=True,
                        stop=True,
                    )

        chunks = J // CHUNK
        first, second, hid = {}, {}, {}

        def product(c, banks, gate, held, name):
            h, lo = divmod(c * CHUNK, HALF)
            held[c] = sb_pool.tile([P, PACK, CHUNK], F32, name=f"{name}{c}", tag=name, bufs=2)
            nc.vector.tensor_tensor(
                held[c][:], banks[h][:, :, lo : lo + CHUNK], gate[:, :, c * CHUNK : (c + 1) * CHUNK], MULT
            )

        def add_up(c):
            hid[c] = tile(f"hid{c}", [P, CHUNK * PACK], BF16)
            nc.vector.tensor_tensor(
                hid[c][:].rearrange("p (c i t) -> p c t i", t=PACK, i=2),
                first[c][:].rearrange("p t (c i) -> p c t i", i=2),
                second[c][:].rearrange("p t (c i) -> p c t i", i=2),
                ADD,
            )

        def finish(c):
            hid_codes = tile(f"hid_codes{c}", [P, CHUNK], U32)
            hid_plane = tile(f"hid_plane{c}", [P, CHUNK], U8)
            nc.vector.quantize_mx(out=hid_codes[:].bitcast(E4M3X4), scales=hid_plane[:], in_=hid[c][:])
            last = c == chunks - 1
            if last:
                p_banks = [psum.tile([P, CHUNK], F32, name=f"p{c}{n}", tag=("p_last", "a0")[n])[:] for n in range(N // P)]
            else:
                p_bank = psum.tile([P, N // P, CHUNK], F32, name=f"p{c}")
                p_banks = [p_bank[:, n, :] for n in range(N // P)]
            for n in range(N // P):
                feats = slice(n * P, (n + 1) * P)
                nc.tensor.matmul_mx(
                    out=p_banks[n],
                    lhsT=wb_codes[:, feats].bitcast(E4M3X4),
                    lhsT_scale=wb_plane[:, feats],
                    rhs=hid_codes[:].bitcast(E4M3X4),
                    rhs_scale=hid_plane[:],
                    start=True,
                    stop=True,
                )
            p_rows = tile(f"p_rows{c}", [P, N // P, CHUNK], F32)
            if last:
                for n in range(N // P):
                    nc.vector.tensor_copy(p_rows[:, n, :], p_banks[n])
            elif c < 2:
                nc.scalar.copy(p_rows[:], p_bank[:])
            else:
                nc.vector.tensor_copy(p_rows[:], p_bank[:])
            places = page_list[:, c * CHUNK // 16 : (c + 1) * CHUNK // 16]
            for n in range(N // P):
                nc.scalar.activation(pages[n][:].indirect(places), p_rows[:, n, :], COPY, scale=so_t[:, n : n + 1])

        product(0, a_banks, ga, first, "first")
        product(0, b_banks, gb, second, "second")
        for c in range(chunks):
            if c + 1 < chunks:
                product(c + 1, a_banks, ga, first, "first")
            add_up(c)
            if c + 1 < chunks:
                product(c + 1, b_banks, gb, second, "second")
            finish(c)

        nc.sync.dma_start(out[0:P, :], pages[0][:])
        nc.scalar.dma_start(out[P : 2 * P, :], pages[1][:])
